import numpy as np
import ml_dtypes


def mxq(x, axis, fmt="e4m3"):
    dtype, down = {"e4m3": (ml_dtypes.float8_e4m3fn, 7), "e5m2": (ml_dtypes.float8_e5m2, 14)}[fmt]
    v = np.moveaxis(np.asarray(x, np.float32).astype(ml_dtypes.bfloat16).astype(np.float64), axis, -1)
    blocks = v.reshape(v.shape[:-1] + (-1, 32))
    amax = np.abs(blocks).max(-1, keepdims=True)
    byte = np.maximum(np.where(amax > 0, np.frexp(amax)[1] - 1 + 127, 0) - down, 1)
    scale = np.exp2(byte - 127.0)
    codes = (blocks / scale).astype(np.float32).astype(dtype).astype(np.float64)
    return np.moveaxis((codes * scale).reshape(v.shape), -1, axis)


WIDE = False


def mx_kscale(k):
    if not WIDE:
        return np.ones(k)
    levels = np.array([10, -10, 5, -5, 0])
    if k % 512:
        return np.exp2(np.random.permutation(np.resize(levels, k // 32))).repeat(32)
    a = np.empty((k // 512, 16))
    for p in range(k // 512):
        a[p, :8] = np.random.permutation(np.resize(levels, 8))
        for g in range(8):
            far = levels[np.abs(levels - a[p, g]) >= 10]
            a[p, g + 8] = far[np.random.randint(len(far))]
    return np.exp2(a.ravel()).repeat(32)


def f64(x):
    return np.asarray(x).astype(np.float64)


def striped(idx):
    return np.tile(idx.reshape(-1, 16).T, (8, 1)).astype(np.uint16)


def unstriped(offs):
    return offs[:16].T.reshape(-1).astype(np.int64)


def relu2(v):
    return np.maximum(v, 0.0) ** 2


K, T, E, C, N = 1024, 768, 12, 256, 128
TOP = 4


def by_expert(wq, xq):
    return np.concatenate([wq[e].T @ xq[:, e * C:(e + 1) * C] for e in range(E)], axis=1)


def setup_inputs():
    n = np.random.standard_normal
    s = mx_kscale(K)[:, None]
    deal = np.repeat(np.arange(E), C).reshape(TOP, T)[:, np.random.permutation(T)]
    deal = np.take_along_axis(deal, np.argsort(np.random.rand(TOP, T), axis=0), axis=0)
    for _ in range(8):
        s_, t_ = np.random.permutation(T).reshape(2, -1); r = np.random.randint(TOP, size=T // 2); x, y = deal[r, s_].copy(), deal[r, t_].copy()
        ok = ~((deal[:, s_] == y).any(0) | (deal[:, t_] == x).any(0)); deal[r[ok], s_[ok]] = y[ok]; deal[r[ok], t_[ok]] = x[ok]
    order = np.lexsort((np.random.rand(TOP * T), deal.reshape(-1)))
    slot_token = order % T; pos = np.empty(TOP * T, np.int64); pos[order] = np.arange(TOP * T); pos = pos.reshape(TOP, T)
    g = np.random.uniform(0.5, 1.5, (TOP, T)); g = g / g.sum(0)
    return {
        "xT": (n((K, T)) * s).astype(np.float32),
        "w": (n((E + 1, K, N)) / np.sqrt(K) / s[None]).astype(np.float32),
        "b": (0.3 * n((N, E + 1))).astype(np.float32),
        "gate": np.stack([np.tile(r, (N, 1)) for r in g]).astype(np.float32),
        "offs": striped(slot_token),
        "pos1": striped(pos[0]),
        "pos2": striped(pos[1]),
        "pos3": striped(pos[2]),
        "pos4": striped(pos[3]),
    }


def reference(xT, w, b, gate, offs, pos1, pos2, pos3, pos4):
    idx = unstriped(offs)
    wq = mxq(f64(w), 1, "e4m3")
    xs = mxq(f64(xT), 0, "e4m3")
    ys = relu2((wq[E].T @ xs) + f64(b)[:, E:])
    xq = mxq(f64(xT)[:, idx], 0, "e4m3")
    y = by_expert(wq, xq)
    y = relu2(y + np.repeat(f64(b)[:, :E], C, axis=1))
    return ys + sum(f64(gate[r]) * y[:, unstriped(p)] for r, p in enumerate((pos1, pos2, pos3, pos4)))

@@ -1,0 +1,212 @@
+from contextlib import ExitStack
+
+import concourse.mybir as mybir
+
+K, T, E, C, N = 1024, 768, 12, 256, 128
+TOP = 4
+FLOPS = 2 * K * N * (E * C + T)
+
+F32 = mybir.dt.float32
+BF16 = mybir.dt.bfloat16
+U32 = mybir.dt.uint32
+U16 = mybir.dt.uint16
+U8 = mybir.dt.uint8
+FP8X4 = mybir.dt.float8_e4m3fn_x4
+ACT = mybir.ActivationFunctionType
+ALU = mybir.AluOpType
+
+P = 128
+PACK = 4
+PASSES = K // (P * PACK)
+GROUPS = [(0, 2), (2, 2), (4, 2), (6, 2), (8, 2), (10, 1), (11, 1)]
+AREA = 1024
+RING = 6
+W_WORDS = PASSES * N * PACK // 2
+FIRST_CUT = 512
+
+
+def slot_at(s):
+    return AREA * (s + s // 2 + 1)
+
+
+def tile_moe_shr_lin_relu2_kernel(tc, xT, w, b, gate, offs, pos1, pos2, pos3, pos4, out):
+    nc = tc.nc
+    with ExitStack() as ctx:
+        keep = ctx.enter_context(tc.tile_pool(name="keep", bufs=1))
+        ring = ctx.enter_context(tc.tile_pool(name="ring", bufs=3))
+        psum = ctx.enter_context(tc.psum_pool(name="psum", bufs=6))
+        psum_s = ctx.enter_context(tc.psum_pool(name="psum_s", bufs=1))
+
+        x_rows = xT.rearrange("(a p h e) t -> a h p e t", a=PASSES, p=P, h=2, e=2)
+        w_rows = w.rearrange("x (a p t) n -> p x a t n", a=PASSES, p=P, t=PACK)
+
+        half = T // 2
+        x_raw = []
+        offs_t = keep.tile([P, E * C // 16], U16, name="offs_t")
+        for a in range(PASSES):
+            for h in range(2):
+                cut = FIRST_CUT if (a, h) == (0, 0) else half
+                for lo, hi in ((0, cut), (cut, T)):
+                    piece = keep.tile([P, 2, hi - lo], F32, name="x_raw%d%d%d" % (a, h, lo))
+                    nc.sync.dma_start(out=piece[:], in_=x_rows[a, h][:, :, lo:hi])
+                    x_raw.append((a, h, lo, hi, piece))
+                if (a, h) == (0, 0):
+                    nc.sync.dma_start(offs_t[:], offs)
+
+        w_raw = {}
+
+        def load_w(e0, ne):
+            w_raw[e0] = keep.tile([P, ne, PASSES, PACK, N], F32, name="w_raw%d" % e0)
+            nc.sync.dma_start(out=w_raw[e0][:], in_=w_rows[:, e0:e0 + ne])
+
+        load_w(*GROUPS[0])
+        bias = keep.tile([P, E + 1], F32, name="bias")
+        nc.sync.dma_start(out=bias[:], in_=b)
+        for grp in GROUPS[1:]:
+            load_w(*grp)
+        load_w(E, 1)
+        pos_t = []
+        for r, pos in enumerate((pos1, pos2, pos3, pos4)):
+            tile_r = keep.tile([P, T // 16], U16, name="pos_t%d" % r)
+            nc.sync.dma_start(tile_r[:], pos)
+            pos_t.append(tile_r)
+        gate_t = keep.tile([P, TOP, T], F32, name="gate_t")
+        nc.sync.dma_start(out=gate_t[:], in_=gate.rearrange("r p t -> p r t"))
+
+        pairs = [keep.tile([P, 2, T], U32, name="pairs%d" % a) for a in range(PASSES)]
+        for a, h, lo, hi, piece in x_raw:
+            dst = pairs[a][:, h, lo:hi].bitcast(BF16).rearrange("p (t e) -> p t e", e=2)
+            src = piece[:].rearrange("p e t -> p t e")
+            if (a, h) == (0, 0):
+                nc.vector.tensor_copy(out=dst, in_=src)
+            else:
+                nc.scalar.activation(out=dst, in_=src, func=ACT.Copy)
+
+        y = keep.tile([P, E * C], F32, name="y")
+        work = keep.tile([P, slot_at(RING - 1) + 2 * T], U32, name="work", align_bytes=64)
+
+        codes, scales, sums = {}, {}, {}
+
+        def cast_w(e0, ne, end):
+            for j in range(ne):
+                for a in range(PASSES):
+                    at = end - (ne - j) * W_WORDS + a * W_WORDS // PASSES
+                    dst = work[:, at:at + W_WORDS // PASSES].bitcast(BF16).rearrange("p (c i t) -> p c t i", i=4, t=PACK)
+                    src = w_raw[e0][:, j, a].rearrange("p t (c i) -> p c t i", i=4)
+                    nc.scalar.copy(out=dst, in_=src)
+
+        def picked(n):
+            ne = GROUPS[n // 2][1]
+            at = slot_at(n % RING)
+            return work[:, at:at + 2 * ne * C].rearrange("p (h s) -> p h s", h=2)
+
+        def gather(n):
+            (e0, ne), a = GROUPS[n // 2], n % 2
+            cols = slice(e0 * C // 16, (e0 + ne) * C // 16)
+            for h in range(2):
+                nc.vector.tensor_copy(picked(n)[:, h, :], pairs[a][:, h, :].indirect(offs_t[:, cols]))
+
+        def interleave(n):
+            ne = GROUPS[n // 2][1]
+            at = slot_at((n - 1) % RING)
+            nc.scalar.copy(out=work[:, at:at + 2 * ne * C].rearrange("p (s h) -> p s h", h=2),
+                           in_=picked(n).rearrange("p h s -> p s h"))
+
+        def quantize(key, lo, hi, tag):
+            width = (hi - lo) // 2
+            pool = keep if tag.startswith("s") else ring
+            codes[key] = pool.tile([P, width], U32, name="codes" + tag, align_bytes=64)
+            scales[key] = pool.tile([P, width], U8, name="scales" + tag, align_bytes=64)
+            nc.vector.quantize_mx(out=codes[key][:].bitcast(FP8X4), scales=scales[key][:], in_=work[:, lo:hi].bitcast(BF16))
+
+        def quantize_unit(n):
+            ne, a = GROUPS[n // 2][1], n % 2
+            at = slot_at((n - 1) % RING)
+            quantize(n, at - a * ne * W_WORDS, at + 2 * ne * C, str(a))
+
+        def multiply(g):
+            ne = GROUPS[g][1]
+            sums[g] = psum.tile([P, ne * C], F32, name="sums")
+            for j in range(ne):
+                for a in range(PASSES):
+                    wc = slice((j * PASSES + a) * N, (j * PASSES + a + 1) * N)
+                    x0 = a * ne * PASSES * N + j * C
+                    xc = slice(x0, x0 + C)
+                    nc.tensor.matmul_mx(
+                        out=sums[g][:, j * C:(j + 1) * C],
+                        lhsT=codes[2 * g + 1][:, wc].bitcast(FP8X4), lhsT_scale=scales[2 * g + 1][:, wc],
+                        rhs=codes[2 * g + a][:, xc].bitcast(FP8X4), rhs_scale=scales[2 * g + a][:, xc],
+                        start=(a == 0), stop=(a == PASSES - 1),
+                    )
+
+        def relu2(g):
+            e0, ne = GROUPS[g]
+            pos_part = ring.tile([P, ne * C], F32, name="pos_part")
+            for j in range(ne):
+                xc = slice(j * C, (j + 1) * C)
+                nc.scalar.activation(out=pos_part[:, xc], in_=sums[g][:, xc], func=ACT.Relu,
+                                     bias=bias[:, e0 + j:e0 + j + 1])
+            nc.scalar.activation(out=y[:, e0 * C:(e0 + ne) * C], in_=pos_part[:], func=ACT.Square)
+
+        units = 2 * len(GROUPS)
+        s_first = slot_at((units - 3) % RING)
+        s_second = slot_at((units - 2) % RING)
+        for n in range(units + 1):
+            if n < units:
+                gather(n)
+                interleave(n)
+                if n % 2 == 1:
+                    cast_w(*GROUPS[n // 2], slot_at((n - 1) % RING))
+                    if n >= 5:
+                        relu2((n - 5) // 2)
+            if n > 0:
+                quantize_unit(n - 1)
+                if n % 2 == 0:
+                    multiply(n // 2 - 1)
+        cast_w(E, 1, s_first)
+        relu2(len(GROUPS) - 2)
+        relu2(len(GROUPS) - 1)
+
+        for a, at in enumerate((s_first, s_second)):
+            nc.vector.tensor_copy(
+                out=work[:, at:at + 2 * T].bitcast(BF16).rearrange("p (t h e) -> p t h e", h=2, e=2),
+                in_=pairs[a][:].rearrange("p h t -> p (h t)").bitcast(BF16).rearrange("p (h t e) -> p t h e", h=2, e=2),
+            )
+        quantize("s0", s_first - W_WORDS, s_first + 2 * T, "s0")
+        quantize("s1", s_second, s_second + 1024, "s1")
+        quantize("s2", s_second + 1024, s_second + 2 * T, "s2")
+        s_pos = keep.tile([P, T], F32, name="s_pos")
+        for lo, hi, key in ((0, 512, "s1"), (512, T, "s2")):
+            s_sums = psum_s.tile([P, hi - lo], F32, name="s_sums%d" % lo)
+            for a in range(PASSES):
+                wc = slice(a * N, (a + 1) * N)
+                xc = slice(PASSES * N + lo, PASSES * N + hi) if a == 0 else slice(0, hi - lo)
+                src = "s0" if a == 0 else key
+                nc.tensor.matmul_mx(
+                    out=s_sums[:], lhsT=codes["s0"][:, wc].bitcast(FP8X4), lhsT_scale=scales["s0"][:, wc],
+                    rhs=codes[src][:, xc].bitcast(FP8X4), rhs_scale=scales[src][:, xc],
+                    start=(a == 0), stop=(a == PASSES - 1),
+                )
+            nc.scalar.activation(out=s_pos[:, lo:hi], in_=s_sums[:], func=ACT.Relu, bias=bias[:, E:E + 1])
+        ys = keep.tile([P, T], F32, name="ys")
+        nc.scalar.activation(out=ys[:], in_=s_pos[:], func=ACT.Square)
+
+        terms = [keep.tile([P, T], F32, name="term%d" % r) for r in range(TOP)]
+        part = [keep.tile([P, T], F32, name="part%d" % r) for r in range(TOP)]
+        toks = [slice(s * half, (s + 1) * half) for s in range(2)]
+        last = TOP - 1
+
+        def weigh(r, lo, hi):
+            nc.vector.tensor_tensor(terms[r][:, lo:hi], y[:].indirect(pos_t[r][:, lo // 16:hi // 16]), gate_t[:, r, lo:hi], ALU.mult)
+
+        for r in range(last):
+            weigh(r, 0, T)
+        nc.vector.tensor_tensor(part[0][:], terms[0][:], terms[1][:], ALU.add)
+        weigh(last, 0, half)
+        nc.vector.tensor_tensor(part[1][:], terms[2][:], ys[:], ALU.add)
+        weigh(last, half, T)
+        for tok in toks:
+            nc.vector.tensor_tensor(part[2][:, tok], part[0][:, tok], part[1][:, tok], ALU.add)
+        for tok in toks:
+            nc.vector.tensor_tensor(part[3][:, tok], part[2][:, tok], terms[last][:, tok], ALU.add)
+            nc.sync.dma_start(out=out[:, tok], in_=part[3][:, tok])

@@ -23,6 +23,7 @@ AREA = 1024
 RING = 6
 W_WORDS = PASSES * N * PACK // 2
 FIRST_CUT = 512
+ON_GPSIMD = (0, 2, 4, 6, 8, 10, 12)
 
 
 def slot_at(s):
@@ -83,17 +84,23 @@ def tile_moe_shr_lin_relu2_kernel(tc, xT, w, b, gate, offs, pos1, pos2, pos3, po
                 nc.scalar.activation(out=dst, in_=src, func=ACT.Copy)
 
         y = keep.tile([P, E * C], F32, name="y")
-        work = keep.tile([P, slot_at(RING - 1) + 2 * T], U32, name="work", align_bytes=64)
+        work = keep.tile([P, slot_at(RING - 1) + AREA], U32, name="work", align_bytes=64)
 
+        shared = keep.tile([P, W_WORDS + PASSES * 2 * T], U32, name="shared", align_bytes=64)
         codes, scales, sums = {}, {}, {}
 
-        def cast_w(e0, ne, end):
+        def cast_w(e0, ne, tile, end):
             for j in range(ne):
                 for a in range(PASSES):
                     at = end - (ne - j) * W_WORDS + a * W_WORDS // PASSES
-                    dst = work[:, at:at + W_WORDS // PASSES].bitcast(BF16).rearrange("p (c i t) -> p c t i", i=4, t=PACK)
-                    src = w_raw[e0][:, j, a].rearrange("p t (c i) -> p c t i", i=4)
-                    nc.scalar.copy(out=dst, in_=src)
+                    dst = tile[:, at:at + W_WORDS // PASSES].bitcast(BF16)
+                    src = w_raw[e0][:, j, a]
+                    if e0 + j in ON_GPSIMD:
+                        nc.gpsimd.tensor_scalar(dst.rearrange("p (n t) -> p n t", t=PACK), src.rearrange("p t n -> p n t"),
+                                                1.0, 0.0, ALU.mult, ALU.add)
+                    else:
+                        nc.scalar.copy(out=dst.rearrange("p (c i t) -> p c t i", i=4, t=PACK),
+                                       in_=src.rearrange("p t (c i) -> p c t i", i=4))
 
         def picked(n):
             ne = GROUPS[n // 2][1]
@@ -112,17 +119,16 @@ def tile_moe_shr_lin_relu2_kernel(tc, xT, w, b, gate, offs, pos1, pos2, pos3, po
             nc.scalar.copy(out=work[:, at:at + 2 * ne * C].rearrange("p (s h) -> p s h", h=2),
                            in_=picked(n).rearrange("p h s -> p s h"))
 
-        def quantize(key, lo, hi, tag):
+        def quantize(key, tile, lo, hi, tag):
             width = (hi - lo) // 2
-            pool = keep if tag.startswith("s") else ring
-            codes[key] = pool.tile([P, width], U32, name="codes" + tag, align_bytes=64)
-            scales[key] = pool.tile([P, width], U8, name="scales" + tag, align_bytes=64)
-            nc.vector.quantize_mx(out=codes[key][:].bitcast(FP8X4), scales=scales[key][:], in_=work[:, lo:hi].bitcast(BF16))
+            codes[key] = ring.tile([P, width], U32, name="codes" + tag, align_bytes=64, bufs=2)
+            scales[key] = ring.tile([P, width], U8, name="scales" + tag, align_bytes=64, bufs=2)
+            nc.vector.quantize_mx(out=codes[key][:].bitcast(FP8X4), scales=scales[key][:], in_=tile[:, lo:hi].bitcast(BF16))
 
         def quantize_unit(n):
             ne, a = GROUPS[n // 2][1], n % 2
             at = slot_at((n - 1) % RING)
-            quantize(n, at - a * ne * W_WORDS, at + 2 * ne * C, str(a))
+            quantize(n, work, at - a * ne * W_WORDS, at + 2 * ne * C, str(a))
 
         def multiply(g):
             ne = GROUPS[g][1]
@@ -149,32 +155,35 @@ def tile_moe_shr_lin_relu2_kernel(tc, xT, w, b, gate, offs, pos1, pos2, pos3, po
             nc.scalar.activation(out=y[:, e0 * C:(e0 + ne) * C], in_=pos_part[:], func=ACT.Square)
 
         units = 2 * len(GROUPS)
-        s_first = slot_at((units - 3) % RING)
-        s_second = slot_at((units - 2) % RING)
+        s_first, s_second = W_WORDS, W_WORDS + 2 * T
+
+        def lay_shared(a):
+            at = W_WORDS + a * 2 * T
+            for lo, hi in ((0, half), (half, T)):
+                nc.scalar.copy(out=shared[:, at + 2 * lo:at + 2 * hi].rearrange("p (t h) -> p t h", h=2),
+                               in_=pairs[a][:, :, lo:hi].rearrange("p h t -> p t h"))
+
         for n in range(units + 1):
             if n < units:
                 gather(n)
                 interleave(n)
                 if n % 2 == 1:
-                    cast_w(*GROUPS[n // 2], slot_at((n - 1) % RING))
+                    cast_w(*GROUPS[n // 2], work, slot_at((n - 1) % RING))
                     if n >= 5:
                         relu2((n - 5) // 2)
+                    if n in (7, 9):
+                        lay_shared((n - 7) // 2)
             if n > 0:
                 quantize_unit(n - 1)
                 if n % 2 == 0:
                     multiply(n // 2 - 1)
-        cast_w(E, 1, s_first)
+        cast_w(E, 1, shared, s_first)
         relu2(len(GROUPS) - 2)
         relu2(len(GROUPS) - 1)
 
-        for a, at in enumerate((s_first, s_second)):
-            nc.vector.tensor_copy(
-                out=work[:, at:at + 2 * T].bitcast(BF16).rearrange("p (t h e) -> p t h e", h=2, e=2),
-                in_=pairs[a][:].rearrange("p h t -> p (h t)").bitcast(BF16).rearrange("p (h t e) -> p t h e", h=2, e=2),
-            )
-        quantize("s0", s_first - W_WORDS, s_first + 2 * T, "s0")
-        quantize("s1", s_second, s_second + 1024, "s1")
-        quantize("s2", s_second + 1024, s_second + 2 * T, "s2")
+        quantize("s1", shared, s_second, s_second + 1024, "0")
+        quantize("s0", shared, s_first - W_WORDS, s_first + 2 * T, "1")
+        quantize("s2", shared, s_second + 1024, s_second + 2 * T, "0")
         s_pos = keep.tile([P, T], F32, name="s_pos")
         for lo, hi, key in ((0, 512, "s1"), (512, T, "s2")):
             s_sums = psum_s.tile([P, hi - lo], F32, name="s_sums%d" % lo)

@@ -1,6 +1,7 @@
 from contextlib import ExitStack
 
 import concourse.mybir as mybir
+from concourse.masks import make_identity
 
 K, T, E, C, N = 1024, 768, 12, 256, 128
 TOP = 4
@@ -19,15 +20,11 @@ P = 128
 PACK = 4
 PASSES = K // (P * PACK)
 GROUPS = [(0, 2), (2, 2), (4, 2), (6, 2), (8, 2), (10, 1), (11, 1)]
-AREA = 1024
-RING = 6
+SLOT = 1024
+SHARE = (0, 128, 128, 128, 128, 128, 0)
 W_WORDS = PASSES * N * PACK // 2
 FIRST_CUT = 512
-ON_GPSIMD = (0, 2, 4, 6, 8, 10, 12)
-
-
-def slot_at(s):
-    return AREA * (s + s // 2 + 1)
+ON_GPSIMD = tuple(range(E))
 
 
 def tile_moe_shr_lin_relu2_kernel(tc, xT, w, b, gate, offs, pos1, pos2, pos3, pos4, out):
@@ -74,6 +71,9 @@ def tile_moe_shr_lin_relu2_kernel(tc, xT, w, b, gate, offs, pos1, pos2, pos3, po
         gate_t = keep.tile([P, TOP, T], F32, name="gate_t")
         nc.sync.dma_start(out=gate_t[:], in_=gate.rearrange("r p t -> p r t"))
 
+        ident = keep.tile([P, P], F32, name="ident")
+        make_identity(nc, ident[:])
+
         pairs = [keep.tile([P, 2, T], U32, name="pairs%d" % a) for a in range(PASSES)]
         for a, h, lo, hi, piece in x_raw:
             dst = pairs[a][:, h, lo:hi].bitcast(BF16).rearrange("p (t e) -> p t e", e=2)
@@ -83,8 +83,13 @@ def tile_moe_shr_lin_relu2_kernel(tc, xT, w, b, gate, offs, pos1, pos2, pos3, po
             else:
                 nc.scalar.activation(out=dst, in_=src, func=ACT.Copy)
 
+        rows = keep.tile([P, PACK, T], BF16, name="rows")
+        for a, h, lo, hi, piece in x_raw:
+            if a == 1:
+                nc.gpsimd.tensor_scalar(rows[:, 2 * h:2 * h + 2, lo:hi], piece[:], 1.0, 0.0, ALU.mult, ALU.add)
+
         y = keep.tile([P, E * C], F32, name="y")
-        work = keep.tile([P, slot_at(RING - 1) + AREA], U32, name="work", align_bytes=64)
+        work = keep.tile([P, 6 * SLOT], U32, name="work", align_bytes=64)
 
         shared = keep.tile([P, W_WORDS + PASSES * 2 * T], U32, name="shared", align_bytes=64)
         codes, scales, sums = {}, {}, {}
@@ -102,22 +107,39 @@ def tile_moe_shr_lin_relu2_kernel(tc, xT, w, b, gate, offs, pos1, pos2, pos3, po
                         nc.scalar.copy(out=dst.rearrange("p (c i t) -> p c t i", i=4, t=PACK),
                                        in_=src.rearrange("p t (c i) -> p c t i", i=4))
 
-        def picked(n):
-            ne = GROUPS[n // 2][1]
-            at = slot_at(n % RING)
-            return work[:, at:at + 2 * ne * C].rearrange("p (h s) -> p h s", h=2)
+        def picked(g, a):
+            ne = GROUPS[g][1]
+            at = 2 * SLOT * (g % 2) if a == 0 else SLOT * (3 + g % 3)
+            count = ne * C - a * SHARE[g]
+            return work[:, at:at + 2 * count].rearrange("p (h s) -> p h s", h=2), count
 
-        def gather(n):
-            (e0, ne), a = GROUPS[n // 2], n % 2
-            cols = slice(e0 * C // 16, (e0 + ne) * C // 16)
+        def laid_at(g, a):
+            ne = GROUPS[g][1]
+            if a == 0:
+                return SLOT * (3 + (g - 1) % 3)
+            return SLOT - 2 * ne * C if g % 2 == 0 else 2 * SLOT
+
+        def w_at(g):
+            return SLOT if g % 2 == 0 else 2 * SLOT - GROUPS[g][1] * W_WORDS
+
+        def gather(g, a):
+            dst, count = picked(g, a)
+            first = GROUPS[g][0] * C
             for h in range(2):
-                nc.vector.tensor_copy(picked(n)[:, h, :], pairs[a][:, h, :].indirect(offs_t[:, cols]))
+                nc.vector.tensor_copy(dst[:, h, :], pairs[a][:, h, :].indirect(offs_t[:, first // 16:(first + count) // 16]))
 
-        def interleave(n):
-            ne = GROUPS[n // 2][1]
-            at = slot_at((n - 1) % RING)
-            nc.scalar.copy(out=work[:, at:at + 2 * ne * C].rearrange("p (s h) -> p s h", h=2),
-                           in_=picked(n).rearrange("p h s -> p s h"))
+        def interleave(g, a):
+            src, count = picked(g, a)
+            at = laid_at(g, a)
+            nc.scalar.copy(out=work[:, at:at + 2 * count].rearrange("p (s h) -> p s h", h=2), in_=src.rearrange("p h s -> p s h"))
+
+        def gather_rows(g):
+            e0, ne = GROUPS[g]
+            end = laid_at(g, 1) + 2 * ne * C
+            dst = work[:, end - 2 * SHARE[g]:end].bitcast(BF16).rearrange("p (s t) -> p s t", t=PACK)
+            stop = (e0 + ne) * C
+            for t in range(PACK):
+                nc.scalar.activation(dst[:, :, t], rows[:, t, :].indirect(offs_t[:, (stop - SHARE[g]) // 16:stop // 16]), ACT.Copy)
 
         def quantize(key, tile, lo, hi, tag):
             width = (hi - lo) // 2
@@ -125,23 +147,24 @@ def tile_moe_shr_lin_relu2_kernel(tc, xT, w, b, gate, offs, pos1, pos2, pos3, po
             scales[key] = ring.tile([P, width], U8, name="scales" + tag, align_bytes=64, bufs=2)
             nc.vector.quantize_mx(out=codes[key][:].bitcast(FP8X4), scales=scales[key][:], in_=tile[:, lo:hi].bitcast(BF16))
 
-        def quantize_unit(n):
-            ne, a = GROUPS[n // 2][1], n % 2
-            at = slot_at((n - 1) % RING)
-            quantize(n, work, at - a * ne * W_WORDS, at + 2 * ne * C, str(a))
+        def quantize_group(g):
+            ne = GROUPS[g][1]
+            quantize((g, 0), work, laid_at(g, 0), laid_at(g, 0) + 2 * ne * C, "0")
+            lo = min(laid_at(g, 1), w_at(g))
+            quantize((g, 1), work, lo, lo + ne * (2 * C + W_WORDS), "1")
 
         def multiply(g):
             ne = GROUPS[g][1]
             sums[g] = psum.tile([P, ne * C], F32, name="sums")
+            w0, x1 = (ne * C, 0) if g % 2 == 0 else (0, ne * PASSES * N)
             for j in range(ne):
                 for a in range(PASSES):
-                    wc = slice((j * PASSES + a) * N, (j * PASSES + a + 1) * N)
-                    x0 = a * ne * PASSES * N + j * C
-                    xc = slice(x0, x0 + C)
+                    wc = slice(w0 + (j * PASSES + a) * N, w0 + (j * PASSES + a + 1) * N)
+                    xc = slice(a * x1 + j * C, a * x1 + (j + 1) * C)
                     nc.tensor.matmul_mx(
                         out=sums[g][:, j * C:(j + 1) * C],
-                        lhsT=codes[2 * g + 1][:, wc].bitcast(FP8X4), lhsT_scale=scales[2 * g + 1][:, wc],
-                        rhs=codes[2 * g + a][:, xc].bitcast(FP8X4), rhs_scale=scales[2 * g + a][:, xc],
+                        lhsT=codes[g, 1][:, wc].bitcast(FP8X4), lhsT_scale=scales[g, 1][:, wc],
+                        rhs=codes[g, a][:, xc].bitcast(FP8X4), rhs_scale=scales[g, a][:, xc],
                         start=(a == 0), stop=(a == PASSES - 1),
                     )
 
@@ -154,7 +177,6 @@ def tile_moe_shr_lin_relu2_kernel(tc, xT, w, b, gate, offs, pos1, pos2, pos3, po
                                      bias=bias[:, e0 + j:e0 + j + 1])
             nc.scalar.activation(out=y[:, e0 * C:(e0 + ne) * C], in_=pos_part[:], func=ACT.Square)
 
-        units = 2 * len(GROUPS)
         s_first, s_second = W_WORDS, W_WORDS + 2 * T
 
         def lay_shared(a):
@@ -163,20 +185,30 @@ def tile_moe_shr_lin_relu2_kernel(tc, xT, w, b, gate, offs, pos1, pos2, pos3, po
                 nc.scalar.copy(out=shared[:, at + 2 * lo:at + 2 * hi].rearrange("p (t h) -> p t h", h=2),
                                in_=pairs[a][:, :, lo:hi].rearrange("p h t -> p t h"))
 
-        for n in range(units + 1):
-            if n < units:
-                gather(n)
-                interleave(n)
-                if n % 2 == 1:
-                    cast_w(*GROUPS[n // 2], work, slot_at((n - 1) % RING))
-                    if n >= 5:
-                        relu2((n - 5) // 2)
-                    if n in (7, 9):
-                        lay_shared((n - 7) // 2)
-            if n > 0:
-                quantize_unit(n - 1)
-                if n % 2 == 0:
-                    multiply(n // 2 - 1)
+        def cast_group(g):
+            cast_w(*GROUPS[g], work, w_at(g) + GROUPS[g][1] * W_WORDS)
+
+        final = len(GROUPS) - 1
+        cast_group(0)
+        for g in range(len(GROUPS)):
+            for a in range(PASSES):
+                gather(g, a)
+                interleave(g, a)
+            if SHARE[g]:
+                gather_rows(g)
+            if g >= 2:
+                relu2(g - 2)
+            if g in (3, 4):
+                lay_shared(g - 3)
+            if g > 0:
+                quantize_group(g - 1)
+                multiply(g - 1)
+                if g < final:
+                    cast_group(g)
+                if g == final - 1:
+                    cast_group(final)
+        quantize_group(final)
+        multiply(final)
         cast_w(E, 1, shared, s_first)
         relu2(len(GROUPS) - 2)
         relu2(len(GROUPS) - 1)
@@ -200,22 +232,39 @@ def tile_moe_shr_lin_relu2_kernel(tc, xT, w, b, gate, offs, pos1, pos2, pos3, po
         ys = keep.tile([P, T], F32, name="ys")
         nc.scalar.activation(out=ys[:], in_=s_pos[:], func=ACT.Square)
 
-        terms = [keep.tile([P, T], F32, name="term%d" % r) for r in range(TOP)]
-        part = [keep.tile([P, T], F32, name="part%d" % r) for r in range(TOP)]
-        toks = [slice(s * half, (s + 1) * half) for s in range(2)]
         last = TOP - 1
+        terms = [keep.tile([P, T], F32, name="term%d" % r) for r in range(TOP)]
+        turned = keep.tile([P, T], F32, name="turned")
+        result = keep.tile([P, T], F32, name="result")
+        blocks = [slice(j * P, (j + 1) * P) for j in range(T // P)]
+        acc = [psum.tile([P, P], F32, name="sums") for blk in blocks]
 
         def weigh(r, lo, hi):
             nc.vector.tensor_tensor(terms[r][:, lo:hi], y[:].indirect(pos_t[r][:, lo // 16:hi // 16]), gate_t[:, r, lo:hi], ALU.mult)
 
-        for r in range(last):
-            weigh(r, 0, T)
-        nc.vector.tensor_tensor(part[0][:], terms[0][:], terms[1][:], ALU.add)
-        weigh(last, 0, half)
-        nc.vector.tensor_tensor(part[1][:], terms[2][:], ys[:], ALU.add)
-        weigh(last, half, T)
-        for tok in toks:
-            nc.vector.tensor_tensor(part[2][:, tok], part[0][:, tok], part[1][:, tok], ALU.add)
-        for tok in toks:
-            nc.vector.tensor_tensor(part[3][:, tok], part[2][:, tok], terms[last][:, tok], ALU.add)
-            nc.sync.dma_start(out=out[:, tok], in_=part[3][:, tok])
+        def add_turned(src, js, start, stop):
+            for j in js:
+                nc.tensor.matmul(acc[j][:], lhsT=src[:, blocks[j]], rhs=ident[:], is_transpose=True, start=start, stop=stop)
+
+        every = range(len(blocks))
+        weigh(0, 0, T)
+        add_turned(terms[0], every, True, False)
+        weigh(1, 0, T)
+        add_turned(terms[1], every, False, False)
+        add_turned(ys, every, False, False)
+        back = []
+        for s, name in enumerate(("s_sums0", "s_sums512")):
+            js = range(s * half // P, (s + 1) * half // P)
+            for part in ([js] if s == 0 else [js[:-1], js[-1:]]):
+                weigh(2, part[0] * P, (part[-1] + 1) * P)
+                add_turned(terms[2], part, False, True)
+            back.append(psum_s.tile([P, half], F32, name=name))
+            for j in js:
+                nc.scalar.copy(out=turned[:, blocks[j]], in_=acc[j][:])
+                nc.tensor.transpose(back[s][:, blocks[j - js[0]]], turned[:, blocks[j]], ident[:])
+        for s in range(2):
+            weigh(last, s * half, (s + 1) * half)
+        for s in range(2):
+            tok = slice(s * half, (s + 1) * half)
+            nc.vector.tensor_tensor(result[:, tok], back[s][:], terms[last][:, tok], ALU.add)
+            nc.sync.dma_start(out=out[:, tok], in_=result[:, tok])

@@ -21,10 +21,10 @@ PACK = 4
 PASSES = K // (P * PACK)
 GROUPS = [(0, 2), (2, 2), (4, 2), (6, 2), (8, 2), (10, 1), (11, 1)]
 SLOT = 1024
-SHARE = (0, 128, 128, 128, 128, 128, 0)
+SHARE = (0, 0, 0, 0, 0, 0, 0)
 W_WORDS = PASSES * N * PACK // 2
 FIRST_CUT = 512
-ON_GPSIMD = tuple(range(E))
+ON_SCALAR = ((1, 1), (3, 1), (5, 1), (7, 1), (9, 1), (11, 0), (11, 1), (12, 0), (12, 1))
 
 
 def tile_moe_shr_lin_relu2_kernel(tc, xT, w, b, gate, offs, pos1, pos2, pos3, pos4, out):
@@ -80,13 +80,10 @@ def tile_moe_shr_lin_relu2_kernel(tc, xT, w, b, gate, offs, pos1, pos2, pos3, po
             src = piece[:].rearrange("p e t -> p t e")
             if (a, h) == (0, 0):
                 nc.vector.tensor_copy(out=dst, in_=src)
+            elif (a, h, lo) > (1, 0, 0):
+                nc.gpsimd.tensor_scalar(dst, src, 1.0, 0.0, ALU.mult, ALU.add)
             else:
                 nc.scalar.activation(out=dst, in_=src, func=ACT.Copy)
-
-        rows = keep.tile([P, PACK, T], BF16, name="rows")
-        for a, h, lo, hi, piece in x_raw:
-            if a == 1:
-                nc.gpsimd.tensor_scalar(rows[:, 2 * h:2 * h + 2, lo:hi], piece[:], 1.0, 0.0, ALU.mult, ALU.add)
 
         y = keep.tile([P, E * C], F32, name="y")
         work = keep.tile([P, 6 * SLOT], U32, name="work", align_bytes=64)
@@ -100,7 +97,7 @@ def tile_moe_shr_lin_relu2_kernel(tc, xT, w, b, gate, offs, pos1, pos2, pos3, po
                     at = end - (ne - j) * W_WORDS + a * W_WORDS // PASSES
                     dst = tile[:, at:at + W_WORDS // PASSES].bitcast(BF16)
                     src = w_raw[e0][:, j, a]
-                    if e0 + j in ON_GPSIMD:
+                    if (e0 + j, a) not in ON_SCALAR:
                         nc.gpsimd.tensor_scalar(dst.rearrange("p (n t) -> p n t", t=PACK), src.rearrange("p t n -> p n t"),
                                                 1.0, 0.0, ALU.mult, ALU.add)
                     else:
@@ -132,14 +129,6 @@ def tile_moe_shr_lin_relu2_kernel(tc, xT, w, b, gate, offs, pos1, pos2, pos3, po
             src, count = picked(g, a)
             at = laid_at(g, a)
             nc.scalar.copy(out=work[:, at:at + 2 * count].rearrange("p (s h) -> p s h", h=2), in_=src.rearrange("p h s -> p s h"))
-
-        def gather_rows(g):
-            e0, ne = GROUPS[g]
-            end = laid_at(g, 1) + 2 * ne * C
-            dst = work[:, end - 2 * SHARE[g]:end].bitcast(BF16).rearrange("p (s t) -> p s t", t=PACK)
-            stop = (e0 + ne) * C
-            for t in range(PACK):
-                nc.scalar.activation(dst[:, :, t], rows[:, t, :].indirect(offs_t[:, (stop - SHARE[g]) // 16:stop // 16]), ACT.Copy)
 
         def quantize(key, tile, lo, hi, tag):
             width = (hi - lo) // 2
@@ -194,8 +183,6 @@ def tile_moe_shr_lin_relu2_kernel(tc, xT, w, b, gate, offs, pos1, pos2, pos3, po
             for a in range(PASSES):
                 gather(g, a)
                 interleave(g, a)
-            if SHARE[g]:
-                gather_rows(g)
             if g >= 2:
                 relu2(g - 2)
             if g in (3, 4):

from contextlib import ExitStack

import concourse.mybir as mybir
from concourse.masks import make_identity

K, T, E, C, N = 1024, 768, 12, 256, 128
TOP = 4
FLOPS = 2 * K * N * (E * C + T)

F32 = mybir.dt.float32
BF16 = mybir.dt.bfloat16
U32 = mybir.dt.uint32
U16 = mybir.dt.uint16
U8 = mybir.dt.uint8
FP8X4 = mybir.dt.float8_e4m3fn_x4
ACT = mybir.ActivationFunctionType
ALU = mybir.AluOpType

P = 128
PACK = 4
PASSES = K // (P * PACK)
GROUPS = [(0, 2), (2, 2), (4, 2), (6, 2), (8, 2), (10, 1), (11, 1)]
SLOT = 1024
SHARE = (0, 0, 0, 0, 0, 0, 0)
W_WORDS = PASSES * N * PACK // 2
FIRST_CUT = 512
ON_SCALAR = ((1, 1), (3, 1), (5, 1), (7, 1), (9, 1), (11, 0), (11, 1), (12, 0), (12, 1))


def tile_moe_shr_lin_relu2_kernel(tc, xT, w, b, gate, offs, pos1, pos2, pos3, pos4, out):
    nc = tc.nc
    with ExitStack() as ctx:
        keep = ctx.enter_context(tc.tile_pool(name="keep", bufs=1))
        ring = ctx.enter_context(tc.tile_pool(name="ring", bufs=3))
        psum = ctx.enter_context(tc.psum_pool(name="psum", bufs=6))
        psum_s = ctx.enter_context(tc.psum_pool(name="psum_s", bufs=1))

        x_rows = xT.rearrange("(a p h e) t -> a h p e t", a=PASSES, p=P, h=2, e=2)
        w_rows = w.rearrange("x (a p t) n -> p x a t n", a=PASSES, p=P, t=PACK)

        half = T // 2
        x_raw = []
        offs_t = keep.tile([P, E * C // 16], U16, name="offs_t")
        for a in range(PASSES):
            for h in range(2):
                cut = FIRST_CUT if (a, h) == (0, 0) else half
                for lo, hi in ((0, cut), (cut, T)):
                    piece = keep.tile([P, 2, hi - lo], F32, name="x_raw%d%d%d" % (a, h, lo))
                    nc.sync.dma_start(out=piece[:], in_=x_rows[a, h][:, :, lo:hi])
                    x_raw.append((a, h, lo, hi, piece))
                if (a, h) == (0, 0):
                    nc.sync.dma_start(offs_t[:], offs)

        w_raw = {}

        def load_w(e0, ne):
            w_raw[e0] = keep.tile([P, ne, PASSES, PACK, N], F32, name="w_raw%d" % e0)
            nc.sync.dma_start(out=w_raw[e0][:], in_=w_rows[:, e0:e0 + ne])

        load_w(*GROUPS[0])
        bias = keep.tile([P, E + 1], F32, name="bias")
        nc.sync.dma_start(out=bias[:], in_=b)
        for grp in GROUPS[1:]:
            load_w(*grp)
        load_w(E, 1)
        pos_t = []
        for r, pos in enumerate((pos1, pos2, pos3, pos4)):
            tile_r = keep.tile([P, T // 16], U16, name="pos_t%d" % r)
            nc.sync.dma_start(tile_r[:], pos)
            pos_t.append(tile_r)
        gate_t = keep.tile([P, TOP, T], F32, name="gate_t")
        nc.sync.dma_start(out=gate_t[:], in_=gate.rearrange("r p t -> p r t"))

        ident = keep.tile([P, P], F32, name="ident")
        make_identity(nc, ident[:])

        pairs = [keep.tile([P, 2, T], U32, name="pairs%d" % a) for a in range(PASSES)]
        for a, h, lo, hi, piece in x_raw:
            dst = pairs[a][:, h, lo:hi].bitcast(BF16).rearrange("p (t e) -> p t e", e=2)
            src = piece[:].rearrange("p e t -> p t e")
            if (a, h) == (0, 0):
                nc.vector.tensor_copy(out=dst, in_=src)
            elif (a, h, lo) > (1, 0, 0):
                nc.gpsimd.tensor_scalar(dst, src, 1.0, 0.0, ALU.mult, ALU.add)
            else:
                nc.scalar.activation(out=dst, in_=src, func=ACT.Copy)

        y = keep.tile([P, E * C], F32, name="y")
        work = keep.tile([P, 6 * SLOT], U32, name="work", align_bytes=64)

        shared = keep.tile([P, W_WORDS + PASSES * 2 * T], U32, name="shared", align_bytes=64)
        codes, scales, sums = {}, {}, {}

        def cast_w(e0, ne, tile, end):
            for j in range(ne):
                for a in range(PASSES):
                    at = end - (ne - j) * W_WORDS + a * W_WORDS // PASSES
                    dst = tile[:, at:at + W_WORDS // PASSES].bitcast(BF16)
                    src = w_raw[e0][:, j, a]
                    if (e0 + j, a) not in ON_SCALAR:
                        nc.gpsimd.tensor_scalar(dst.rearrange("p (n t) -> p n t", t=PACK), src.rearrange("p t n -> p n t"),
                                                1.0, 0.0, ALU.mult, ALU.add)
                    else:
                        nc.scalar.copy(out=dst.rearrange("p (c i t) -> p c t i", i=4, t=PACK),
                                       in_=src.rearrange("p t (c i) -> p c t i", i=4))

        def picked(g, a):
            ne = GROUPS[g][1]
            at = 2 * SLOT * (g % 2) if a == 0 else SLOT * (3 + g % 3)
            count = ne * C - a * SHARE[g]
            return work[:, at:at + 2 * count].rearrange("p (h s) -> p h s", h=2), count

        def laid_at(g, a):
            ne = GROUPS[g][1]
            if a == 0:
                return SLOT * (3 + (g - 1) % 3)
            return SLOT - 2 * ne * C if g % 2 == 0 else 2 * SLOT

        def w_at(g):
            return SLOT if g % 2 == 0 else 2 * SLOT - GROUPS[g][1] * W_WORDS

        def gather(g, a):
            dst, count = picked(g, a)
            first = GROUPS[g][0] * C
            for h in range(2):
                nc.vector.tensor_copy(dst[:, h, :], pairs[a][:, h, :].indirect(offs_t[:, first // 16:(first + count) // 16]))

        def interleave(g, a):
            src, count = picked(g, a)
            at = laid_at(g, a)
            nc.scalar.copy(out=work[:, at:at + 2 * count].rearrange("p (s h) -> p s h", h=2), in_=src.rearrange("p h s -> p s h"))

        def quantize(key, tile, lo, hi, tag):
            width = (hi - lo) // 2
            codes[key] = ring.tile([P, width], U32, name="codes" + tag, align_bytes=64, bufs=2)
            scales[key] = ring.tile([P, width], U8, name="scales" + tag, align_bytes=64, bufs=2)
            nc.vector.quantize_mx(out=codes[key][:].bitcast(FP8X4), scales=scales[key][:], in_=tile[:, lo:hi].bitcast(BF16))

        def quantize_group(g):
            ne = GROUPS[g][1]
            quantize((g, 0), work, laid_at(g, 0), laid_at(g, 0) + 2 * ne * C, "0")
            lo = min(laid_at(g, 1), w_at(g))
            quantize((g, 1), work, lo, lo + ne * (2 * C + W_WORDS), "1")

        def multiply(g):
            ne = GROUPS[g][1]
            sums[g] = psum.tile([P, ne * C], F32, name="sums")
            w0, x1 = (ne * C, 0) if g % 2 == 0 else (0, ne * PASSES * N)
            for j in range(ne):
                for a in range(PASSES):
                    wc = slice(w0 + (j * PASSES + a) * N, w0 + (j * PASSES + a + 1) * N)
                    xc = slice(a * x1 + j * C, a * x1 + (j + 1) * C)
                    nc.tensor.matmul_mx(
                        out=sums[g][:, j * C:(j + 1) * C],
                        lhsT=codes[g, 1][:, wc].bitcast(FP8X4), lhsT_scale=scales[g, 1][:, wc],
                        rhs=codes[g, a][:, xc].bitcast(FP8X4), rhs_scale=scales[g, a][:, xc],
                        start=(a == 0), stop=(a == PASSES - 1),
                    )

        def relu2(g):
            e0, ne = GROUPS[g]
            pos_part = ring.tile([P, ne * C], F32, name="pos_part")
            for j in range(ne):
                xc = slice(j * C, (j + 1) * C)
                nc.scalar.activation(out=pos_part[:, xc], in_=sums[g][:, xc], func=ACT.Relu,
                                     bias=bias[:, e0 + j:e0 + j + 1])
            nc.scalar.activation(out=y[:, e0 * C:(e0 + ne) * C], in_=pos_part[:], func=ACT.Square)

        s_first, s_second = W_WORDS, W_WORDS + 2 * T

        def lay_shared(a):
            at = W_WORDS + a * 2 * T
            for lo, hi in ((0, half), (half, T)):
                nc.scalar.copy(out=shared[:, at + 2 * lo:at + 2 * hi].rearrange("p (t h) -> p t h", h=2),
                               in_=pairs[a][:, :, lo:hi].rearrange("p h t -> p t h"))

        def cast_group(g):
            cast_w(*GROUPS[g], work, w_at(g) + GROUPS[g][1] * W_WORDS)

        final = len(GROUPS) - 1
        cast_group(0)
        for g in range(len(GROUPS)):
            for a in range(PASSES):
                gather(g, a)
                interleave(g, a)
            if g >= 2:
                relu2(g - 2)
            if g in (3, 4):
                lay_shared(g - 3)
            if g > 0:
                quantize_group(g - 1)
                multiply(g - 1)
                if g < final:
                    cast_group(g)
                if g == final - 1:
                    cast_group(final)
        quantize_group(final)
        multiply(final)
        cast_w(E, 1, shared, s_first)
        relu2(len(GROUPS) - 2)
        relu2(len(GROUPS) - 1)

        quantize("s1", shared, s_second, s_second + 1024, "0")
        quantize("s0", shared, s_first - W_WORDS, s_first + 2 * T, "1")
        quantize("s2", shared, s_second + 1024, s_second + 2 * T, "0")
        s_pos = keep.tile([P, T], F32, name="s_pos")
        for lo, hi, key in ((0, 512, "s1"), (512, T, "s2")):
            s_sums = psum_s.tile([P, hi - lo], F32, name="s_sums%d" % lo)
            for a in range(PASSES):
                wc = slice(a * N, (a + 1) * N)
                xc = slice(PASSES * N + lo, PASSES * N + hi) if a == 0 else slice(0, hi - lo)
                src = "s0" if a == 0 else key
                nc.tensor.matmul_mx(
                    out=s_sums[:], lhsT=codes["s0"][:, wc].bitcast(FP8X4), lhsT_scale=scales["s0"][:, wc],
                    rhs=codes[src][:, xc].bitcast(FP8X4), rhs_scale=scales[src][:, xc],
                    start=(a == 0), stop=(a == PASSES - 1),
                )
            nc.scalar.activation(out=s_pos[:, lo:hi], in_=s_sums[:], func=ACT.Relu, bias=bias[:, E:E + 1])
        ys = keep.tile([P, T], F32, name="ys")
        nc.scalar.activation(out=ys[:], in_=s_pos[:], func=ACT.Square)

        last = TOP - 1
        terms = [keep.tile([P, T], F32, name="term%d" % r) for r in range(TOP)]
        turned = keep.tile([P, T], F32, name="turned")
        result = keep.tile([P, T], F32, name="result")
        blocks = [slice(j * P, (j + 1) * P) for j in range(T // P)]
        acc = [psum.tile([P, P], F32, name="sums") for blk in blocks]

        def weigh(r, lo, hi):
            nc.vector.tensor_tensor(terms[r][:, lo:hi], y[:].indirect(pos_t[r][:, lo // 16:hi // 16]), gate_t[:, r, lo:hi], ALU.mult)

        def add_turned(src, js, start, stop):
            for j in js:
                nc.tensor.matmul(acc[j][:], lhsT=src[:, blocks[j]], rhs=ident[:], is_transpose=True, start=start, stop=stop)

        every = range(len(blocks))
        weigh(0, 0, T)
        add_turned(terms[0], every, True, False)
        weigh(1, 0, T)
        add_turned(terms[1], every, False, False)
        add_turned(ys, every, False, False)
        back = []
        for s, name in enumerate(("s_sums0", "s_sums512")):
            js = range(s * half // P, (s + 1) * half // P)
            for part in ([js] if s == 0 else [js[:-1], js[-1:]]):
                weigh(2, part[0] * P, (part[-1] + 1) * P)
                add_turned(terms[2], part, False, True)
            back.append(psum_s.tile([P, half], F32, name=name))
            for j in js:
                nc.scalar.copy(out=turned[:, blocks[j]], in_=acc[j][:])
                nc.tensor.transpose(back[s][:, blocks[j - js[0]]], turned[:, blocks[j]], ident[:])
        for s in range(2):
            weigh(last, s * half, (s + 1) * half)
        for s in range(2):
            tok = slice(s * half, (s + 1) * half)
            nc.vector.tensor_tensor(result[:, tok], back[s][:], terms[last][:, tok], ALU.add)
            nc.sync.dma_start(out=out[:, tok], in_=result[:, tok])
